import numpy as np, ml_dtypes
CORES = [66,74,82,90,194,202,210,218]
N = 8
import mx_ref
BF = ml_dtypes.bfloat16
def entries(a):
    return np.ascontiguousarray(a.T).reshape(-1)
def table(e):
    return np.ascontiguousarray(np.reshape(e, (-1, 16)).T).astype(np.int32)
def cols(t, e):
    v = np.concatenate([t.reshape(128, -1, 4), np.zeros((128, 1, 4), BF)], axis=1)
    return np.ascontiguousarray(v[:, e]).reshape(128, -1)
def f(rng, *shape):
    return mx_ref.flush((rng.standard_normal(shape, dtype=np.float32) * np.exp2(rng.integers(-2, 3, shape[:-1] + (1,)))).astype(BF))
def wide(rng, *shape, cols=0):
    v = rng.standard_normal(shape, dtype=np.float32) * np.exp2(rng.integers(-12, 13, shape)).astype(np.float32)
    if cols: v *= np.repeat(np.exp2(rng.integers(-cols, cols + 1, shape[:-2] + (1, shape[-1] // 4))) * (rng.random(shape[:-2] + (1, shape[-1] // 4)) > 0.0625), 4, axis=-1).astype(np.float32)
    return mx_ref.flush(v.astype(BF))
T, S, CAPP, CL, K, O = 128, 256, 32, 48, 1024, 2
H = 65536 // (N * K)
def counts(rng, tot, cap, lead=None, least=2):
    n = np.full(N, least)
    if lead is not None:
        for i in range(N):
            q = (lead + i) % N; n[q] += min(cap - n[q], tot - n.sum())
    while n.sum() < tot:
        q = rng.integers(0, N)
        if n[q] < cap: n[q] += 1
    return n
def lists(rng, full=False, hot=False, other=False, few=False):
    a, b = rng.integers(1, N, 2); z = rng.integers(0, N); least = 0 if full else 2
    n = np.stack([counts(rng, T, CAPP, (r + a) % N if full or other else z if hot else None, least) for r in range(N)])
    part, pool = [], []
    for q in range(N):
        c = n[:, q].sum(); p = rng.permutation(K)[:c]
        key = q + N * (p + K * rng.integers(0, H, c))
        part.append(np.split(key, np.cumsum(n[:, q])[:-1])); pool.append(rng.choice(key, 1) if few else key)
    has = [np.concatenate([part[q][r] for q in range(N)]) for r in range(N)]
    ky, lk = [], []
    for r in range(N):
        ky.append(table(rng.permutation(has[r])))
        if other:
            s = (r + a) % N; e = rng.permutation(has[s])[:S]; m = np.bincount(e & (N - 1), minlength=N); e = [e]
            for q in ((s + a) % N, (s + a + 1) % N):
                more = rng.permutation(np.setdiff1d(pool[q], part[q][s]))[:CL - m[q]]
                e.append(more); m[q] += len(more)
            while m.sum() < S:
                q = rng.integers(0, N)
                if m[q] < CL: m[q] += 1; e.append(rng.choice(part[q][s], 1))
            u = np.unique(np.concatenate(e)); lead = part[(s + a) % N][s]
            assert len(lead) == CAPP and np.isin(lead, u).all()
            assert any(q != r and m[q] == CL and ((u & (N - 1)) == q).sum() == CL for q in range(N))
        else:
            m = counts(rng, S, CL, (r + b) % N if full else z if hot else None, least)
            e = [rng.choice(pool[q], m[q]) for q in range(N)]
        lk.append(table(rng.permutation(np.concatenate(e))))
    return {"ky": np.stack(ky), "lk": np.stack(lk)}
def setup_inputs(rng):
    d = lists(rng)
    return {"x": f(rng, N, 128, 4 * T), "ky": d["ky"], "lk": d["lk"], "w": f(rng, N, 128, 512 * O)}
def setup_inputs_full(rng):
    return {**setup_inputs(rng), **lists(rng, full=True)}
def setup_inputs_hot(rng):
    return {**setup_inputs(rng), **lists(rng, hot=True)}
def setup_inputs_other(rng):
    return {**setup_inputs(rng), **lists(rng, other=True)}
def setup_inputs_repeats(rng):
    return {**setup_inputs(rng), **lists(rng, few=True)}
def setup_inputs_spread(rng):
    d = setup_inputs(rng); d["x"] = wide(rng, N, 128, 4 * T, cols=8); return d
def check_inputs(d):
    b = []
    keys = np.stack([entries(d["ky"][r]) for r in range(N)]).astype(np.int64)
    if keys.min() < 0 or keys.max() > 65535: b.append("ky")
    if len(np.unique(keys & (N * K - 1))) != N * T: b.append("owner and place")
    for r in range(N):
        l = entries(d["lk"][r]).astype(np.int64)
        if np.bincount(keys[r] & (N - 1), minlength=N).max() > CAPP: b.append("CAPP")
        if not np.isin(l, keys).all(): b.append("lk")
        if np.bincount(l & (N - 1), minlength=N).max() > CL: b.append("CL")
    return b
def reference(x, ky, lk, w):
    every = np.concatenate([x[r] for r in range(N)], axis=1)
    number = np.full(65536, -1); number[np.concatenate([entries(ky[r]) for r in range(N)])] = np.arange(N * T)
    y = np.zeros((N, 128, O * S), np.float32)
    for r in range(N):
        v = mx_ref.quantize(cols(every, number[entries(lk[r])]))
        for o in range(O): y[r][:, S * o:S * o + S] = mx_ref.matmul(mx_ref.quantize(np.ascontiguousarray(w[r][:, 512 * o:512 * o + 512])), v)
    return {"y": y}

@@ -1,0 +1,236 @@
+from concourse.bass import DstId, RemoteDMATransfer
+from concourse.mybir import dt, AluOpType, ActivationFunctionType
+
+TC, S, O, NK = 128, 256, 2, 8192
+HALF = 4
+Z = 16
+WIN = HALF * TC + Z
+OWN = (HALF - 1) * TC
+MID = 256
+COPIES = 4
+F0, F1, FV = 1024, 2048, 5632
+FA = 1536
+B = 128
+
+SCRATCH = {
+    "kd": ("dram", [2 * COPIES * 2, 128, 1], "int32"),
+    "ld": ("dram", [2, 128, 1], "int32"),
+    "rd": ("dram", [COPIES * 2, 128, 1], "int32"),
+    "kq": ("sbuf", [128, 32], "int32"),
+    "kqa": ("sbuf", [128, 32], "int32"),
+    "ko": ("sbuf", [128, 32], "uint16"),
+    "lo": ("sbuf", [128, 16], "int32"),
+    "loa": ("sbuf", [128, 16], "int32"),
+    "loo": ("sbuf", [128, 16], "uint16"),
+    "tb": ("sbuf", [128, NK], "bfloat16"),
+    "vals": ("sbuf", [128, 2 * TC], "bfloat16"),
+    "pi": ("sbuf", [128, 1], "int32"),
+    "pia": ("sbuf", [128, 1], "int32"),
+    "npm": ("sbuf", [128, 1], "float32"),
+    "ri": ("sbuf", [128, S], "bfloat16"),
+    "rs": ("sbuf", [128, S], "bfloat16"),
+    "md": ("sbuf", [128, S], "bfloat16"),
+    "mk": ("sbuf", [128, S], "bfloat16"),
+    "g1": ("sbuf", [128, S], "bfloat16"),
+    "c1": ("sbuf", [128, S], "bfloat16"),
+    "t1": ("sbuf", [64, 16], "float32"),
+    "of1": ("sbuf", [128, 16], "uint16"),
+    "g2": ("sbuf", [128, S], "bfloat16"),
+    "c2": ("sbuf", [128, S], "bfloat16"),
+    "t2": ("sbuf", [64, 16], "float32"),
+    "of2": ("sbuf", [128, 16], "uint16"),
+    "xt": ("sbuf", [128, 4 * (TC + Z)], "bfloat16"),
+    "wt": ("sbuf", [128, 512 * O], "bfloat16"),
+    "wq": ("sbuf", [128, 128 * O], "float8_e4m3fn_x4"),
+    "wp": ("sbuf", [128, 128 * O], "uint8"),
+    "win": ("sbuf", [128, WIN], "float8_e4m3fn_x4"),
+    "sw": ("sbuf", [128, WIN], "uint8"),
+    "sl": ("sbuf", [128, S], "float8_e4m3fn_x4"),
+    "sp": ("sbuf", [128, S], "uint8"),
+    "hc": ("sbuf", [128, S], "float8_e4m3fn_x4"),
+    "hp": ("sbuf", [128, S], "uint8"),
+    "arc": ("sbuf", [128, S], "float8_e4m3fn_x4"),
+    "arp": ("sbuf", [128, S], "uint8"),
+    "y0": ("sbuf", [128, S], "float32"),
+    "y1": ("sbuf", [128, S], "float32"),
+    "ps": ("psum", [128, 2048], "float32"),
+}
+SEMAPHORES = ["ll", "lc", "xl", "wl", "ol", "kl", "kar", "rar", "car", "sar", "car2", "sar2", "snt",
+              "ipi", "iri", "ival", "vz", "vt0", "vt1", "vt2", "af0", "af1", "vpi", "vnp", "vva", "ars", "amd", "amk",
+              "vq", "vw", "voa", "voo", "vka", "vko", "vsc", "vg1", "vc1", "ve1", "vo1", "vp1", "vg2", "vc2", "ve2", "vo2", "vp2",
+              "sp1", "sp2", "mm0", "mm1", "mm2", "mm3", "cv0", "cv1", "ca0", "ca1", "st"]
+
+
+def rank_program(g, core, T, topo):
+    if T.rank_of(core) is None:
+        return
+    s, v, a, p, y = T.sem, g.vector, g.scalar, g.tensor, g.sync
+    ACT = ActivationFunctionType
+    half = [c for c in T.cores if topo.host(c) == topo.host(core)]
+    peers = [c for c in half if c != core]
+    partner = [c for c in T.cores if topo.host(c) != topo.host(core) and topo.chip(c) == topo.chip(core)][0]
+
+    def slot(c):
+        return (half.index(c) ^ half.index(core)) - 1
+
+    def kpos(sl, copy):
+        return (sl // 2 * COPIES + copy) * 2 + sl % 2
+
+    def dst(c):
+        rid, pid = topo.addr(c, core)
+        return DstId(rid=rid, pnc=pid)
+
+    mask3 = topo.mask(core, peers[0])
+    for c in peers:
+        mask3 &= topo.mask(core, c)
+    maskp = topo.mask(core, partner)
+    eng = [e for e in topo.engines(core, partner) if mask3 >> e & 1]
+    n3 = len([e for e in range(16) if mask3 >> e & 1])
+    n_p = len(topo.engines(core, partner))
+
+    y.dma_start(T.kd[kpos(HALF - 1, 0), :, 0], T.ky[:]).then_inc(s.ll, 16)
+    a.dma_start(T.ld[:, :, 0], T.lk[:]).then_inc(s.ll, 16)
+    a.dma_start(T.xt[:, 0:4 * TC], T.x[:]).then_inc(s.xl, 16)
+    for k in range(1, COPIES):
+        y.dma_start(T.kd[kpos(HALF - 1, k), :, 0], T.ky[:]).then_inc(s.lc, 16)
+    y.dma_start(T.wt[:], T.w[:]).then_inc(s.wl, 16)
+    for b in range(8):
+        y.dma_start(T.lo[16 * b:16 * b + 16, :], T.lk[:]).then_inc(s.ol, 16)
+
+    def vals(m):
+        g.iota(T.vals[:, 128 * m:128 * m + 128], [[16, 8], [128, 2], [2, 8]], m - MID, 0,
+               allow_small_or_imprecise_dtypes=True).then_inc(s.ival, 1)
+    g.iota(T.pi[:], [[0, 1]], 0, 1).then_inc(s.ipi, 1)
+    vals(0)
+    g.wait_ge(s.ll, 32)
+    lists = []
+    for k in range(0, COPIES, 2):
+        to = [(c, u) for u in (k, k + 1) for c in peers]
+        lists.append(RemoteDMATransfer(dst_ids=[dst(c) for c, u in to], dma_engine_mask=1 << eng[k], remote_sem=s.kar,
+                                       srcs=[T.kd[kpos(HALF - 1, 0)]], dsts=[T.kd[kpos(slot(c), u)] for c, u in to]))
+    for h in range(2):
+        lists.append(RemoteDMATransfer(dst_ids=[dst(partner) for u in range(COPIES)], dma_engine_mask=1 << eng[4 + 2 * h],
+                                       remote_sem=s.rar, srcs=[T.ld[h]], dsts=[T.rd[2 * u + h] for u in range(COPIES)]))
+    g.remote_dma_fused(lists, local_sem=s.snt)
+    g.wait_ge(s.vq, 1)
+    g.remote_dma_fused([
+        RemoteDMATransfer(dst_ids=[dst(c) for c in peers], dma_engine_mask=mask3, remote_sem=s.car,
+                          srcs=[T.win[:, OWN:OWN + TC].bitcast(dt.uint8)],
+                          dsts=[T.win[:, TC * slot(c):TC * slot(c) + TC].bitcast(dt.uint8) for c in peers]),
+    ], local_sem=s.snt)
+    g.remote_dma_fused([
+        RemoteDMATransfer(dst_ids=[dst(c) for c in peers], dma_engine_mask=mask3, remote_sem=s.sar,
+                          srcs=[T.sw[:, OWN:OWN + TC]],
+                          dsts=[T.sw[:, TC * slot(c):TC * slot(c) + TC] for c in peers]),
+    ], local_sem=s.snt)
+    vals(1)
+    g.iota(T.ri[:], [[0, 16], [1, 16]], 0, 0, allow_small_or_imprecise_dtypes=True).then_inc(s.iri, 1)
+    rid, pid = topo.addr(partner, core)
+    g.wait_ge(s.vp1, 1)
+    g.remote_dma(T.arc[:].bitcast(dt.uint8), T.sl[:].bitcast(dt.uint8), s.car2, s.snt, pid, rid, maskp)
+    g.wait_ge(s.sp1, 1)
+    g.remote_dma(T.arp[:], T.sp[:], s.sar2, s.snt, pid, rid, maskp)
+
+    y.wait_ge(s.kar, COPIES * len(peers))
+    y.dma_start(T.kq[0:64, 0:16], T.kd[0:2 * COPIES, :, 0]).then_inc(s.kl, 16)
+    y.wait_ge(s.ll, 32)
+    y.wait_ge(s.lc, 16 * (COPIES - 1))
+    y.dma_start(T.kq[64:128, 0:16], T.kd[2 * COPIES:4 * COPIES, :, 0]).then_inc(s.kl, 16)
+    y.wait_ge(s.rar, 2 * COPIES)
+    for h in range(2):
+        y.dma_start(T.kq[64 * h:64 * h + 64, 16:32], T.rd[:, :, 0]).then_inc(s.kl, 16)
+
+    fill = float(HALF * TC - MID)
+    v.memset(T.tb[:, 0:F0], fill).then_inc(s.vt0, 1)
+    v.memset(T.xt[:, 4 * TC:4 * (TC + Z)], 0.0).then_inc(s.vz, 1)
+    v.memset(T.tb[:, F0:F1], fill).then_inc(s.vt1, 1)
+    v.wait_ge(s.vz, 1)
+    v.wait_ge(s.xl, 16)
+    v.quantize_mx(T.win[:, OWN:WIN], T.sw[:, OWN:WIN], T.xt[:]).then_inc(s.vq, 1)
+    v.wait_ge(s.ipi, 1)
+    v.tensor_scalar(T.pia[:], T.pi[:], 15, None, AluOpType.bitwise_and).then_inc(s.vpi, 1)
+    v.memset(T.tb[:, F1:FV], fill).then_inc(s.vt2, 1)
+    v.wait_ge(s.vpi, 1)
+    v.tensor_scalar(T.npm[:], T.pia[:], -1.0, None, AluOpType.mult).then_inc(s.vnp, 1)
+    v.wait_ge(s.ival, 2)
+    v.tensor_scalar(T.vals[64:128, :], T.vals[64:128, :], float(2 * TC), None, AluOpType.add).then_inc(s.vva, 1)
+    v.wait_ge(s.kl, 64)
+    v.tensor_scalar(T.kqa[:], T.kq[:], NK - 1, None, AluOpType.bitwise_and).then_inc(s.vka, 1)
+    v.wait_ge(s.vka, 1)
+    v.tensor_copy(T.ko[:], T.kqa[:]).then_inc(s.vko, 1)
+    for q in (s.vt0, s.vt1, s.vt2, s.af0, s.af1, s.vva, s.vko):
+        v.wait_ge(q, 1)
+    v.tensor_copy(T.tb[:, 0:NK].indirect(T.ko[:, 0:16]), T.vals[:]).then_inc(s.vsc, 1)
+    v.wait_ge(s.amk, 1)
+    v.wait_ge(s.ars, 1)
+    v.wait_ge(s.vsc, 1)
+
+    def offsets(keys, gx, cx, tx, of, sg, sc, se, so):
+        v.tensor_tensor(gx[:], T.tb[:, 0:NK].indirect(keys), T.mk[:], AluOpType.mult).then_inc(sg, 1)
+        v.wait_ge(sg, 1)
+        v.tensor_tensor_scan(cx[:], T.rs[:], gx[:], 0.0, AluOpType.mult, AluOpType.add).then_inc(sc, 1)
+        v.wait_ge(sc, 1)
+        v.tensor_tensor(tx[0:64, :], cx[0:64, 15:S:16], cx[64:128, 15:S:16], AluOpType.add).then_inc(se, 1)
+        v.wait_ge(se, 1)
+        v.tensor_copy(of[0:64, :], tx[0:64, :]).then_inc(so, 1)
+        v.tensor_copy(of[64:128, :], tx[0:64, :]).then_inc(so, 1)
+
+    offsets(T.ko[:, 16:32], T.g1, T.c1, T.t1, T.of1, s.vg1, s.vc1, s.ve1, s.vo1)
+    v.wait_ge(s.vq, 1)
+    v.wait_ge(s.car, n3 * len(peers))
+    v.wait_ge(s.vo1, 2)
+    v.tensor_copy(T.sl[:, 0:S].bitcast(dt.uint32), T.win[:, 0:WIN].bitcast(dt.uint32).indirect(T.of1[:, 0:16])).then_inc(s.vp1, 1)
+    v.wait_ge(s.ol, 128)
+    v.tensor_scalar(T.loa[:], T.lo[:], NK - 1, None, AluOpType.bitwise_and).then_inc(s.voa, 1)
+    v.wait_ge(s.wl, 16)
+    v.quantize_mx(T.wq[:], T.wp[:], T.wt[:]).then_inc(s.vw, 1)
+    v.wait_ge(s.voa, 1)
+    v.tensor_copy(T.loo[:], T.loa[:]).then_inc(s.voo, 1)
+    v.wait_ge(s.voo, 1)
+    offsets(T.loo[:, 0:16], T.g2, T.c2, T.t2, T.of2, s.vg2, s.vc2, s.ve2, s.vo2)
+    v.wait_ge(s.vo2, 2)
+    v.tensor_copy(T.hc[:, 0:S].bitcast(dt.uint32), T.win[:, 0:WIN].bitcast(dt.uint32).indirect(T.of2[:, 0:16])).then_inc(s.vp2, 1)
+
+    a.wait_ge(s.vt0, 1)
+    a.activation(T.tb[:, FV:FV + F0], T.tb[:, 0:F0], ACT.Copy).then_inc(s.af0, 1)
+    a.wait_ge(s.vt1, 1)
+    a.activation(T.tb[:, FV + F0:NK], T.tb[:, 0:FA], ACT.Copy).then_inc(s.af1, 1)
+    a.wait_ge(s.iri, 1)
+    a.wait_ge(s.vnp, 1)
+    a.activation(T.md[:], T.ri[:], ACT.Abs, bias=T.npm[:]).then_inc(s.amd, 1)
+    a.activation(T.rs[:], T.ri[:], ACT.Sign).then_inc(s.ars, 1)
+    a.wait_ge(s.amd, 1)
+    a.activation(T.mk[:], T.md[:], ACT.Relu, bias=1.0, scale=-1.0).then_inc(s.amk, 1)
+    a.wait_ge(s.vq, 1)
+    a.wait_ge(s.sar, n3 * len(peers))
+    a.wait_ge(s.vo1, 2)
+    a.activation(T.sp[:, 0:S], T.sw[:, 0:WIN].indirect(T.of1[:, 0:16]), ACT.Copy).then_inc(s.sp1, 1)
+    a.wait_ge(s.vo2, 2)
+    a.activation(T.hp[:, 0:S], T.sw[:, 0:WIN].indirect(T.of2[:, 0:16]), ACT.Copy).then_inc(s.sp2, 1)
+
+    def product(q, codes, scales, first):
+        o, h = q // 2, q % 2
+        return p.matmul_mx(T.ps[:, 512 * q:512 * q + B], T.wq[:, 128 * o:128 * o + 128], T.wp[:, 128 * o:128 * o + 128],
+                           codes[:, B * h:B * h + B], scales[:, B * h:B * h + B], first, not first)
+    p.wait_ge(s.vw, 1)
+    p.wait_ge(s.vp2, 1)
+    p.wait_ge(s.sp2, 1)
+    for q in range(2 * O):
+        product(q, T.hc, T.hp, True)
+    p.wait_ge(s.car2, n_p)
+    p.wait_ge(s.sar2, n_p)
+    for q in range(2 * O):
+        product(q, T.arc, T.arp, False).then_inc(s["mm%d" % q], 1)
+    for o in range(O):
+        yo = T["y%d" % o]
+        v.wait_ge(s["mm%d" % (2 * o)], 1)
+        v.tensor_copy(yo[:, 0:B], T.ps[:, 1024 * o:1024 * o + B]).then_inc(s["cv%d" % o], 1)
+        a.wait_ge(s["mm%d" % (2 * o + 1)], 1)
+        a.activation(yo[:, B:S], T.ps[:, 1024 * o + 512:1024 * o + 512 + B], ACT.Copy).then_inc(s["ca%d" % o], 1)
+    for o in range(O):
+        q = (y, a)[o]
+        q.wait_ge(s["cv%d" % o], 1)
+        q.wait_ge(s["ca%d" % o], 1)
+        q.dma_start(T.y[:, S * o:S * o + S], T["y%d" % o][:]).then_inc(s.st, 16)
+    y.wait_ge(s.st, 32)
+    g.wait_ge(s.snt, len(lists) + 2 * n3 + 2 * n_p)

@@ -7,38 +7,19 @@ Z = 16
 WIN = HALF * TC + Z
 OWN = (HALF - 1) * TC
 MID = 256
-COPIES = 4
-F0, F1, FV = 1024, 2048, 5632
-FA = 1536
 B = 128
+F0, F1, FV = 512, 2048, 5504
+FA = FV + F0 + (NK - FV - F0) // 2
 
 SCRATCH = {
-    "kd": ("dram", [2 * COPIES * 2, 128, 1], "int32"),
+    "kd": ("dram", [2 * HALF, 128, 1], "int32"),
     "ld": ("dram", [2, 128, 1], "int32"),
-    "rd": ("dram", [COPIES * 2, 128, 1], "int32"),
-    "kq": ("sbuf", [128, 32], "int32"),
-    "kqa": ("sbuf", [128, 32], "int32"),
-    "ko": ("sbuf", [128, 32], "uint16"),
-    "lo": ("sbuf", [128, 16], "int32"),
-    "loa": ("sbuf", [128, 16], "int32"),
-    "loo": ("sbuf", [128, 16], "uint16"),
+    "rd": ("dram", [2 * HALF, 128, 1], "int32"),
+    "kq": ("sbuf", [128, 24], "int32"),
+    "kqa": ("sbuf", [128, 24], "int32"),
+    "ko": ("sbuf", [128, 40], "uint16"),
     "tb": ("sbuf", [128, NK], "bfloat16"),
-    "vals": ("sbuf", [128, 2 * TC], "bfloat16"),
-    "pi": ("sbuf", [128, 1], "int32"),
-    "pia": ("sbuf", [128, 1], "int32"),
-    "npm": ("sbuf", [128, 1], "float32"),
-    "ri": ("sbuf", [128, S], "bfloat16"),
-    "rs": ("sbuf", [128, S], "bfloat16"),
-    "md": ("sbuf", [128, S], "bfloat16"),
-    "mk": ("sbuf", [128, S], "bfloat16"),
-    "g1": ("sbuf", [128, S], "bfloat16"),
-    "c1": ("sbuf", [128, S], "bfloat16"),
-    "t1": ("sbuf", [64, 16], "float32"),
-    "of1": ("sbuf", [128, 16], "uint16"),
-    "g2": ("sbuf", [128, S], "bfloat16"),
-    "c2": ("sbuf", [128, S], "bfloat16"),
-    "t2": ("sbuf", [64, 16], "float32"),
-    "of2": ("sbuf", [128, 16], "uint16"),
+    "vals": ("sbuf", [128, TC], "bfloat16"),
     "xt": ("sbuf", [128, 4 * (TC + Z)], "bfloat16"),
     "wt": ("sbuf", [128, 512 * O], "bfloat16"),
     "wq": ("sbuf", [128, 128 * O], "float8_e4m3fn_x4"),
@@ -51,94 +32,100 @@ SCRATCH = {
     "hp": ("sbuf", [128, S], "uint8"),
     "arc": ("sbuf", [128, S], "float8_e4m3fn_x4"),
     "arp": ("sbuf", [128, S], "uint8"),
-    "y0": ("sbuf", [128, S], "float32"),
-    "y1": ("sbuf", [128, S], "float32"),
+    "yb": ("sbuf", [128, O * S], "float32"),
     "ps": ("psum", [128, 2048], "float32"),
 }
-SEMAPHORES = ["ll", "lc", "xl", "wl", "ol", "kl", "kar", "rar", "car", "sar", "car2", "sar2", "snt",
-              "ipi", "iri", "ival", "vz", "vt0", "vt1", "vt2", "af0", "af1", "vpi", "vnp", "vva", "ars", "amd", "amk",
-              "vq", "vw", "voa", "voo", "vka", "vko", "vsc", "vg1", "vc1", "ve1", "vo1", "vp1", "vg2", "vc2", "ve2", "vo2", "vp2",
-              "sp1", "sp2", "mm0", "mm1", "mm2", "mm3", "cv0", "cv1", "ca0", "ca1", "st"]
+for n in (1, 2):
+    SCRATCH["g%d" % n] = ("sbuf", [128, S], "bfloat16")
+    SCRATCH["t%d" % n] = ("sbuf", [128, S], "bfloat16")
+    SCRATCH["u%d" % n] = ("sbuf", [64, 16], "float32")
+    SCRATCH["w%d" % n] = ("sbuf", [64, 16], "float32")
+    SCRATCH["of%d" % n] = ("sbuf", [128, 16], "uint16")
+SEMAPHORES = ["ll", "lc", "xl", "wl", "ol", "kl", "go", "kar", "rar", "car", "sar", "ca0", "ca1", "sa", "snt",
+              "ival", "vz", "vt0", "vt1", "vt2", "af", "vq", "vw", "vka", "vk", "vl", "vsc", "vg1", "ag1", "ag2",
+              "vt_1", "vu1", "vw1", "vo1", "vt_2", "vu2", "vw2", "vo2", "vp0", "vp1", "as1", "vh0", "vh1", "ah0", "ah1",
+              "mm0", "mm1", "mm2", "mm3", "cp0", "cp1", "cp2", "cp3", "st"]
 
 
 def rank_program(g, core, T, topo):
     if T.rank_of(core) is None:
         return
     s, v, a, p, y = T.sem, g.vector, g.scalar, g.tensor, g.sync
-    ACT = ActivationFunctionType
+    ACT, ALU = ActivationFunctionType, AluOpType
     half = [c for c in T.cores if topo.host(c) == topo.host(core)]
     peers = [c for c in half if c != core]
+    far = [c for c in peers if not topo.mates(c, core) and not topo.same_plane(c, core)]
+    near = [c for c in peers if c not in far]
     partner = [c for c in T.cores if topo.host(c) != topo.host(core) and topo.chip(c) == topo.chip(core)][0]
 
     def slot(c):
         return (half.index(c) ^ half.index(core)) - 1
 
-    def kpos(sl, copy):
-        return (sl // 2 * COPIES + copy) * 2 + sl % 2
-
     def dst(c):
         rid, pid = topo.addr(c, core)
         return DstId(rid=rid, pnc=pid)
 
-    mask3 = topo.mask(core, peers[0])
+    mask = topo.mask(core, partner)
     for c in peers:
-        mask3 &= topo.mask(core, c)
-    maskp = topo.mask(core, partner)
-    eng = [e for e in topo.engines(core, partner) if mask3 >> e & 1]
-    n3 = len([e for e in range(16) if mask3 >> e & 1])
-    n_p = len(topo.engines(core, partner))
+        mask &= topo.mask(core, c)
+    eng = [e for e in topo.engines(core, partner) if mask >> e & 1]
+    ne = len(eng)
+    sent = [0]
 
-    y.dma_start(T.kd[kpos(HALF - 1, 0), :, 0], T.ky[:]).then_inc(s.ll, 16)
-    a.dma_start(T.ld[:, :, 0], T.lk[:]).then_inc(s.ll, 16)
+    def send(to, src, dsts, sem):
+        g.remote_dma_fused([RemoteDMATransfer(dst_ids=[dst(c) for c in to], dma_engine_mask=mask, remote_sem=sem,
+                                              srcs=[src], dsts=dsts)], local_sem=s.snt)
+        sent[0] += ne
+
+    def u8(view):
+        return view.bitcast(dt.uint8)
+
+    def u32(view):
+        return view.bitcast(dt.uint32)
+
+    y.dma_start(T.kd[2 * HALF - 2, :, 0], T.ky[:]).then_inc(s.ll, 16)
+    a.dma_start(T.ld[0, :, 0], T.lk[:, 0:8]).then_inc(s.ll, 16)
+    y.dma_start(T.ld[1, :, 0], T.lk[:, 8:16]).then_inc(s.ll, 16)
     a.dma_start(T.xt[:, 0:4 * TC], T.x[:]).then_inc(s.xl, 16)
-    for k in range(1, COPIES):
-        y.dma_start(T.kd[kpos(HALF - 1, k), :, 0], T.ky[:]).then_inc(s.lc, 16)
+    y.dma_start(T.kd[2 * HALF - 1, :, 0], T.ky[:]).then_inc(s.lc, 16)
     y.dma_start(T.wt[:], T.w[:]).then_inc(s.wl, 16)
-    for b in range(8):
-        y.dma_start(T.lo[16 * b:16 * b + 16, :], T.lk[:]).then_inc(s.ol, 16)
+    y.wait_ge(s.ll, 48)
+    for q in range(HALF):
+        y.dma_start(T.kq[32 * q:32 * q + 32, 16:24], T.ld[:, :, 0]).then_inc(s.ol, 16)
 
-    def vals(m):
-        g.iota(T.vals[:, 128 * m:128 * m + 128], [[16, 8], [128, 2], [2, 8]], m - MID, 0,
-               allow_small_or_imprecise_dtypes=True).then_inc(s.ival, 1)
-    g.iota(T.pi[:], [[0, 1]], 0, 1).then_inc(s.ipi, 1)
+    def vals(q):
+        g.iota(T.vals[32 * q:32 * q + 32, :], [[1, TC]], TC * q - MID, 0, allow_small_or_imprecise_dtypes=True).then_inc(s.ival, 1)
     vals(0)
-    g.wait_ge(s.ll, 32)
-    lists = []
-    for k in range(0, COPIES, 2):
-        to = [(c, u) for u in (k, k + 1) for c in peers]
-        lists.append(RemoteDMATransfer(dst_ids=[dst(c) for c, u in to], dma_engine_mask=1 << eng[k], remote_sem=s.kar,
-                                       srcs=[T.kd[kpos(HALF - 1, 0)]], dsts=[T.kd[kpos(slot(c), u)] for c, u in to]))
-    for h in range(2):
-        lists.append(RemoteDMATransfer(dst_ids=[dst(partner) for u in range(COPIES)], dma_engine_mask=1 << eng[4 + 2 * h],
-                                       remote_sem=s.rar, srcs=[T.ld[h]], dsts=[T.rd[2 * u + h] for u in range(COPIES)]))
-    g.remote_dma_fused(lists, local_sem=s.snt)
-    g.wait_ge(s.vq, 1)
-    g.remote_dma_fused([
-        RemoteDMATransfer(dst_ids=[dst(c) for c in peers], dma_engine_mask=mask3, remote_sem=s.car,
-                          srcs=[T.win[:, OWN:OWN + TC].bitcast(dt.uint8)],
-                          dsts=[T.win[:, TC * slot(c):TC * slot(c) + TC].bitcast(dt.uint8) for c in peers]),
-    ], local_sem=s.snt)
-    g.remote_dma_fused([
-        RemoteDMATransfer(dst_ids=[dst(c) for c in peers], dma_engine_mask=mask3, remote_sem=s.sar,
-                          srcs=[T.sw[:, OWN:OWN + TC]],
-                          dsts=[T.sw[:, TC * slot(c):TC * slot(c) + TC] for c in peers]),
-    ], local_sem=s.snt)
     vals(1)
-    g.iota(T.ri[:], [[0, 16], [1, 16]], 0, 0, allow_small_or_imprecise_dtypes=True).then_inc(s.iri, 1)
-    rid, pid = topo.addr(partner, core)
+    g.wait_ge(s.ll, 48)
+    lists = []
+    for e in range(2):
+        lists.append(RemoteDMATransfer(dst_ids=[dst(c) for c in far + near], dma_engine_mask=1 << eng[2 * e], remote_sem=s.kar,
+                                       srcs=[T.kd[2 * HALF - 2]], dsts=[T.kd[2 * slot(c) + e] for c in far + near]))
+        lists.append(RemoteDMATransfer(dst_ids=[dst(partner)] * HALF, dma_engine_mask=1 << eng[4 + 2 * e],
+                                       remote_sem=s.rar, srcs=[T.ld[e]], dsts=[T.rd[2 * q + e] for q in range(HALF)]))
+    g.remote_dma_fused(lists, local_sem=s.snt)
+    sent[0] += len(lists)
+    g.wait_ge(s.vq, 1)
+    send(far, u8(T.win[:, OWN:OWN + TC]), [u8(T.win[:, TC * slot(c):TC * slot(c) + TC]) for c in far], s.car)
+    vals(2)
+    vals(3)
+    g.wait_ge(s.go, 1)
+    send(near, u8(T.win[:, OWN:OWN + TC]), [u8(T.win[:, TC * slot(c):TC * slot(c) + TC]) for c in near], s.car)
+    send(far + near, T.sw[:, OWN:OWN + TC], [T.sw[:, TC * slot(c):TC * slot(c) + TC] for c in far + near], s.sar)
+    g.wait_ge(s.vp0, 1)
+    send([partner], u8(T.sl[:, 0:B]), [u8(T.arc[:, 0:B])], s.ca0)
+    g.wait_ge(s.as1, 2)
+    send([partner], T.sp[:], [T.arp[:]], s.sa)
     g.wait_ge(s.vp1, 1)
-    g.remote_dma(T.arc[:].bitcast(dt.uint8), T.sl[:].bitcast(dt.uint8), s.car2, s.snt, pid, rid, maskp)
-    g.wait_ge(s.sp1, 1)
-    g.remote_dma(T.arp[:], T.sp[:], s.sar2, s.snt, pid, rid, maskp)
+    send([partner], u8(T.sl[:, B:S]), [u8(T.arc[:, B:S])], s.ca1)
 
-    y.wait_ge(s.kar, COPIES * len(peers))
-    y.dma_start(T.kq[0:64, 0:16], T.kd[0:2 * COPIES, :, 0]).then_inc(s.kl, 16)
-    y.wait_ge(s.ll, 32)
-    y.wait_ge(s.lc, 16 * (COPIES - 1))
-    y.dma_start(T.kq[64:128, 0:16], T.kd[2 * COPIES:4 * COPIES, :, 0]).then_inc(s.kl, 16)
-    y.wait_ge(s.rar, 2 * COPIES)
-    for h in range(2):
-        y.dma_start(T.kq[64 * h:64 * h + 64, 16:32], T.rd[:, :, 0]).then_inc(s.kl, 16)
+    y.wait_ge(s.lc, 16)
+    y.wait_ge(s.kar, 2 * len(peers))
+    y.dma_start(T.kq[:, 0:8], T.kd[:, :, 0]).then_inc(s.kl, 16)
+    y.wait_ge(s.rar, 2 * HALF)
+    y.dma_start(T.kq[:, 8:16], T.rd[:, :, 0]).then_inc(s.kl, 16)
+    y.sem_inc(s.go, 1)
 
     fill = float(HALF * TC - MID)
     v.memset(T.tb[:, 0:F0], fill).then_inc(s.vt0, 1)
@@ -147,90 +134,103 @@ def rank_program(g, core, T, topo):
     v.wait_ge(s.vz, 1)
     v.wait_ge(s.xl, 16)
     v.quantize_mx(T.win[:, OWN:WIN], T.sw[:, OWN:WIN], T.xt[:]).then_inc(s.vq, 1)
-    v.wait_ge(s.ipi, 1)
-    v.tensor_scalar(T.pia[:], T.pi[:], 15, None, AluOpType.bitwise_and).then_inc(s.vpi, 1)
     v.memset(T.tb[:, F1:FV], fill).then_inc(s.vt2, 1)
-    v.wait_ge(s.vpi, 1)
-    v.tensor_scalar(T.npm[:], T.pia[:], -1.0, None, AluOpType.mult).then_inc(s.vnp, 1)
-    v.wait_ge(s.ival, 2)
-    v.tensor_scalar(T.vals[64:128, :], T.vals[64:128, :], float(2 * TC), None, AluOpType.add).then_inc(s.vva, 1)
-    v.wait_ge(s.kl, 64)
-    v.tensor_scalar(T.kqa[:], T.kq[:], NK - 1, None, AluOpType.bitwise_and).then_inc(s.vka, 1)
-    v.wait_ge(s.vka, 1)
-    v.tensor_copy(T.ko[:], T.kqa[:]).then_inc(s.vko, 1)
-    for q in (s.vt0, s.vt1, s.vt2, s.af0, s.af1, s.vva, s.vko):
-        v.wait_ge(q, 1)
-    v.tensor_copy(T.tb[:, 0:NK].indirect(T.ko[:, 0:16]), T.vals[:]).then_inc(s.vsc, 1)
-    v.wait_ge(s.amk, 1)
-    v.wait_ge(s.ars, 1)
-    v.wait_ge(s.vsc, 1)
-
-    def offsets(keys, gx, cx, tx, of, sg, sc, se, so):
-        v.tensor_tensor(gx[:], T.tb[:, 0:NK].indirect(keys), T.mk[:], AluOpType.mult).then_inc(sg, 1)
-        v.wait_ge(sg, 1)
-        v.tensor_tensor_scan(cx[:], T.rs[:], gx[:], 0.0, AluOpType.mult, AluOpType.add).then_inc(sc, 1)
-        v.wait_ge(sc, 1)
-        v.tensor_tensor(tx[0:64, :], cx[0:64, 15:S:16], cx[64:128, 15:S:16], AluOpType.add).then_inc(se, 1)
-        v.wait_ge(se, 1)
-        v.tensor_copy(of[0:64, :], tx[0:64, :]).then_inc(so, 1)
-        v.tensor_copy(of[64:128, :], tx[0:64, :]).then_inc(so, 1)
-
-    offsets(T.ko[:, 16:32], T.g1, T.c1, T.t1, T.of1, s.vg1, s.vc1, s.ve1, s.vo1)
-    v.wait_ge(s.vq, 1)
-    v.wait_ge(s.car, n3 * len(peers))
-    v.wait_ge(s.vo1, 2)
-    v.tensor_copy(T.sl[:, 0:S].bitcast(dt.uint32), T.win[:, 0:WIN].bitcast(dt.uint32).indirect(T.of1[:, 0:16])).then_inc(s.vp1, 1)
-    v.wait_ge(s.ol, 128)
-    v.tensor_scalar(T.loa[:], T.lo[:], NK - 1, None, AluOpType.bitwise_and).then_inc(s.voa, 1)
     v.wait_ge(s.wl, 16)
     v.quantize_mx(T.wq[:], T.wp[:], T.wt[:]).then_inc(s.vw, 1)
-    v.wait_ge(s.voa, 1)
-    v.tensor_copy(T.loo[:], T.loa[:]).then_inc(s.voo, 1)
-    v.wait_ge(s.voo, 1)
-    offsets(T.loo[:, 0:16], T.g2, T.c2, T.t2, T.of2, s.vg2, s.vc2, s.ve2, s.vo2)
-    v.wait_ge(s.vo2, 2)
-    v.tensor_copy(T.hc[:, 0:S].bitcast(dt.uint32), T.win[:, 0:WIN].bitcast(dt.uint32).indirect(T.of2[:, 0:16])).then_inc(s.vp2, 1)
+    v.wait_ge(s.ol, 16 * HALF)
+    v.wait_ge(s.kl, 32)
+    v.tensor_scalar(T.kqa[:], T.kq[:], NK - 1, None, ALU.bitwise_and).then_inc(s.vka, 1)
+    v.wait_ge(s.vka, 1)
+    v.tensor_copy(T.ko[:, 0:8], T.kqa[:, 0:8]).then_inc(s.vk, 1)
+    for h in range(2):
+        v.tensor_copy(T.ko[:, 8 + h:40:2], T.kqa[:, 8:24]).then_inc(s.vl, 1)
+    for q, n in ((s.vt0, 1), (s.vt1, 1), (s.vt2, 1), (s.af, 3), (s.ival, HALF), (s.vk, 1)):
+        v.wait_ge(q, n)
+    v.tensor_copy(T.tb[:].indirect(T.ko[:, 0:8]), T.vals[:]).then_inc(s.vsc, 1)
+    v.wait_ge(s.vl, 2)
+    v.wait_ge(s.vsc, 1)
+    v.tensor_copy(T.g1[:, 0:B], T.tb[:].indirect(T.ko[:, 8:16])).then_inc(s.vg1, 1)
+
+    def turn(n):
+        v.transpose(T["t%d" % n][:], T["g%d" % n][:]).then_inc(s["vt_%d" % n], 1)
+
+    def offsets(n):
+        t, u, w, of = T["t%d" % n], T["u%d" % n], T["w%d" % n], T["of%d" % n]
+        v.wait_ge(s["vt_%d" % n], 1)
+        for e in range(2):
+            v.tensor_tensor(u[:, 8 * e:8 * e + 8], t[0:64, 16 * e:S:32], t[64:128, 16 * e:S:32], ALU.min).then_inc(s["vu%d" % n], 1)
+        v.wait_ge(s["vu%d" % n], 2)
+        for h in range(2):
+            v.tensor_tensor(w[32 * h:32 * h + 32, :], u[0:32, :], u[32:64, :], ALU.min).then_inc(s["vw%d" % n], 1)
+        v.wait_ge(s["vw%d" % n], 2)
+        for h in range(2):
+            v.tensor_scalar(of[64 * h:64 * h + 64, :], w[:], float(MID), None, ALU.add).then_inc(s["vo%d" % n], 1)
+        v.wait_ge(s["vo%d" % n], 2)
+
+    def pick(out, of, h):
+        return v.tensor_copy(u32(out[:, B * h:B * h + B]), u32(T.win[:]).indirect(of[:, 8 * h:8 * h + 8]))
+
+    v.wait_ge(s.vg1, 1)
+    v.wait_ge(s.ag1, 1)
+    turn(1)
+    offsets(1)
+    v.wait_ge(s.vq, 1)
+    v.wait_ge(s.car, ne * len(peers))
+    pick(T.sl, T.of1, 0).then_inc(s.vp0, 1)
+    v.wait_ge(s.ag2, 1)
+    turn(2)
+    pick(T.sl, T.of1, 1).then_inc(s.vp1, 1)
+    offsets(2)
+    for h in range(2):
+        pick(T.hc, T.of2, h).then_inc(s["vh%d" % h], 1)
 
     a.wait_ge(s.vt0, 1)
-    a.activation(T.tb[:, FV:FV + F0], T.tb[:, 0:F0], ACT.Copy).then_inc(s.af0, 1)
+    a.activation(T.tb[:, FV:FV + F0], T.tb[:, 0:F0], ACT.Copy).then_inc(s.af, 1)
     a.wait_ge(s.vt1, 1)
-    a.activation(T.tb[:, FV + F0:NK], T.tb[:, 0:FA], ACT.Copy).then_inc(s.af1, 1)
-    a.wait_ge(s.iri, 1)
-    a.wait_ge(s.vnp, 1)
-    a.activation(T.md[:], T.ri[:], ACT.Abs, bias=T.npm[:]).then_inc(s.amd, 1)
-    a.activation(T.rs[:], T.ri[:], ACT.Sign).then_inc(s.ars, 1)
-    a.wait_ge(s.amd, 1)
-    a.activation(T.mk[:], T.md[:], ACT.Relu, bias=1.0, scale=-1.0).then_inc(s.amk, 1)
-    a.wait_ge(s.vq, 1)
-    a.wait_ge(s.sar, n3 * len(peers))
-    a.wait_ge(s.vo1, 2)
-    a.activation(T.sp[:, 0:S], T.sw[:, 0:WIN].indirect(T.of1[:, 0:16]), ACT.Copy).then_inc(s.sp1, 1)
-    a.wait_ge(s.vo2, 2)
-    a.activation(T.hp[:, 0:S], T.sw[:, 0:WIN].indirect(T.of2[:, 0:16]), ACT.Copy).then_inc(s.sp2, 1)
+    a.activation(T.tb[:, FV + F0:FA], T.tb[:, 0:FA - FV - F0], ACT.Copy).then_inc(s.af, 1)
+    a.activation(T.tb[:, FA:NK], T.tb[:, 0:NK - FA], ACT.Copy).then_inc(s.af, 1)
+    a.wait_ge(s.vl, 2)
+    a.wait_ge(s.vsc, 1)
+    a.activation(T.g1[:, B:S], T.tb[:].indirect(T.ko[:, 16:24]), ACT.Copy).then_inc(s.ag1, 1)
+    a.activation(T.g2[:], T.tb[:].indirect(T.ko[:, 24:40]), ACT.Copy).then_inc(s.ag2, 1)
 
-    def product(q, codes, scales, first):
-        o, h = q // 2, q % 2
+    def pick_scales(out, of, h):
+        return a.activation(out[:, B * h:B * h + B], T.sw[:].indirect(of[:, 8 * h:8 * h + 8]), ACT.Copy)
+    a.wait_ge(s.vq, 1)
+    a.wait_ge(s.sar, ne * len(peers))
+    a.wait_ge(s.vo1, 2)
+    for h in range(2):
+        pick_scales(T.sp, T.of1, h).then_inc(s.as1, 1)
+    a.wait_ge(s.vo2, 2)
+    for h in range(2):
+        pick_scales(T.hp, T.of2, h).then_inc(s["ah%d" % h], 1)
+
+    def product(o, h, codes, scales, first):
+        q = 2 * h + o
         return p.matmul_mx(T.ps[:, 512 * q:512 * q + B], T.wq[:, 128 * o:128 * o + 128], T.wp[:, 128 * o:128 * o + 128],
                            codes[:, B * h:B * h + B], scales[:, B * h:B * h + B], first, not first)
     p.wait_ge(s.vw, 1)
-    p.wait_ge(s.vp2, 1)
-    p.wait_ge(s.sp2, 1)
+    for h in range(2):
+        p.wait_ge(s["vh%d" % h], 1)
+        p.wait_ge(s["ah%d" % h], 1)
+        for o in range(O):
+            product(o, h, T.hc, T.hp, True)
+        p.wait_ge(s["ca%d" % h], ne)
+        if h == 0:
+            p.wait_ge(s.sa, ne)
+        for o in range(O):
+            product(o, h, T.arc, T.arp, False).then_inc(s["mm%d" % (2 * h + o)], 1)
     for q in range(2 * O):
-        product(q, T.hc, T.hp, True)
-    p.wait_ge(s.car2, n_p)
-    p.wait_ge(s.sar2, n_p)
-    for q in range(2 * O):
-        product(q, T.arc, T.arp, False).then_inc(s["mm%d" % q], 1)
-    for o in range(O):
-        yo = T["y%d" % o]
-        v.wait_ge(s["mm%d" % (2 * o)], 1)
-        v.tensor_copy(yo[:, 0:B], T.ps[:, 1024 * o:1024 * o + B]).then_inc(s["cv%d" % o], 1)
-        a.wait_ge(s["mm%d" % (2 * o + 1)], 1)
-        a.activation(yo[:, B:S], T.ps[:, 1024 * o + 512:1024 * o + 512 + B], ACT.Copy).then_inc(s["ca%d" % o], 1)
-    for o in range(O):
-        q = (y, a)[o]
-        q.wait_ge(s["cv%d" % o], 1)
-        q.wait_ge(s["ca%d" % o], 1)
-        q.dma_start(T.y[:, S * o:S * o + S], T["y%d" % o][:]).then_inc(s.st, 16)
-    y.wait_ge(s.st, 32)
-    g.wait_ge(s.snt, len(lists) + 2 * n3 + 2 * n_p)
+        h, o = q // 2, q % 2
+        out = T.yb[:, S * o + B * h:S * o + B * h + B]
+        if o == 0:
+            v.wait_ge(s["mm%d" % q], 1)
+            v.tensor_copy(out, T.ps[:, 512 * q:512 * q + B]).then_inc(s["cp%d" % q], 1)
+        else:
+            a.wait_ge(s["mm%d" % q], 1)
+            a.activation(out, T.ps[:, 512 * q:512 * q + B], ACT.Copy).then_inc(s["cp%d" % q], 1)
+        z = a if q == 2 * O - 1 else y
+        z.wait_ge(s["cp%d" % q], 1)
+        z.dma_start(T.y[:, S * o + B * h:S * o + B * h + B], out).then_inc(s.st, 16)
+    y.wait_ge(s.st, 32 * O)
+    g.wait_ge(s.snt, sent[0])

@@ -12,9 +12,9 @@ F0, F1, FV = 512, 2048, 5504
 FA = FV + F0 + (NK - FV - F0) // 2
 
 SCRATCH = {
-    "kd": ("dram", [2 * HALF, 128, 1], "int32"),
-    "ld": ("dram", [2, 128, 1], "int32"),
-    "rd": ("dram", [2 * HALF, 128, 1], "int32"),
+    "kd": ("dram", [HALF, 128, 2], "int32"),
+    "ld": ("dram", [128, 2], "int32"),
+    "rd": ("dram", [HALF, 128, 2], "int32"),
     "kq": ("sbuf", [128, 24], "int32"),
     "kqa": ("sbuf", [128, 24], "int32"),
     "ko": ("sbuf", [128, 40], "uint16"),
@@ -41,7 +41,7 @@ for n in (1, 2):
     SCRATCH["u%d" % n] = ("sbuf", [64, 16], "float32")
     SCRATCH["w%d" % n] = ("sbuf", [64, 16], "float32")
     SCRATCH["of%d" % n] = ("sbuf", [128, 16], "uint16")
-SEMAPHORES = ["ll", "lc", "xl", "wl", "ol", "kl", "go", "kar", "rar", "car", "sar", "ca0", "ca1", "sa", "snt",
+SEMAPHORES = ["ll", "xl", "wl", "ol", "kl", "rl", "vla", "go", "kar", "rar", "car", "sar", "ca0", "ca1", "sa", "snt",
               "ival", "vz", "vt0", "vt1", "vt2", "af", "vq", "vw", "vka", "vk", "vl", "vsc", "vg1", "ag1", "ag2",
               "vt_1", "vu1", "vw1", "vo1", "vt_2", "vu2", "vw2", "vo2", "vp0", "vp1", "as1", "vh0", "vh1", "ah0", "ah1",
               "mm0", "mm1", "mm2", "mm3", "cp0", "cp1", "cp2", "cp3", "st"]
@@ -52,14 +52,13 @@ def rank_program(g, core, T, topo):
         return
     s, v, a, p, y = T.sem, g.vector, g.scalar, g.tensor, g.sync
     ACT, ALU = ActivationFunctionType, AluOpType
-    half = [c for c in T.cores if topo.host(c) == topo.host(core)]
-    peers = [c for c in half if c != core]
-    far = [c for c in peers if not topo.mates(c, core) and not topo.same_plane(c, core)]
-    near = [c for c in peers if c not in far]
-    partner = [c for c in T.cores if topo.host(c) != topo.host(core) and topo.chip(c) == topo.chip(core)][0]
+    half = [c for c in T.cores if c == core or topo.same_plane(c, core)]
+    partner = [c for c in T.cores if topo.mates(c, core)][0]
 
     def slot(c):
         return (half.index(c) ^ half.index(core)) - 1
+    peers = sorted([c for c in half if c != core], key=slot)
+    far, near = peers[:1], peers[1:]
 
     def dst(c):
         rid, pid = topo.addr(c, core)
@@ -83,27 +82,24 @@ def rank_program(g, core, T, topo):
     def u32(view):
         return view.bitcast(dt.uint32)
 
-    y.dma_start(T.kd[2 * HALF - 2, :, 0], T.ky[:]).then_inc(s.ll, 16)
-    a.dma_start(T.ld[0, :, 0], T.lk[:, 0:8]).then_inc(s.ll, 16)
-    y.dma_start(T.ld[1, :, 0], T.lk[:, 8:16]).then_inc(s.ll, 16)
-    a.dma_start(T.xt[:, 0:4 * TC], T.x[:]).then_inc(s.xl, 16)
-    y.dma_start(T.kd[2 * HALF - 1, :, 0], T.ky[:]).then_inc(s.lc, 16)
+    for e, q in enumerate((y, a)):
+        q.dma_start(T.ld[64 * e:64 * e + 64, :], T.lk[:, 8 * e:8 * e + 8]).then_inc(s.ll, 16)
+        q.dma_start(T.kd[HALF - 1, 64 * e:64 * e + 64, :], T.ky[:]).then_inc(s.ll, 16)
+    y.dma_start(T.xt[:, 0:4 * TC], T.x[:]).then_inc(s.xl, 16)
     y.dma_start(T.wt[:], T.w[:]).then_inc(s.wl, 16)
-    y.wait_ge(s.ll, 48)
+    y.wait_ge(s.ll, 64)
     for q in range(HALF):
-        y.dma_start(T.kq[32 * q:32 * q + 32, 16:24], T.ld[:, :, 0]).then_inc(s.ol, 16)
+        y.dma_start(T.kq[32 * q:32 * q + 32, 16:24], T.ld[:]).then_inc(s.ol, 16)
 
     def vals(q):
         g.iota(T.vals[32 * q:32 * q + 32, :], [[1, TC]], TC * q - MID, 0, allow_small_or_imprecise_dtypes=True).then_inc(s.ival, 1)
     vals(0)
     vals(1)
-    g.wait_ge(s.ll, 48)
-    lists = []
-    for e in range(2):
-        lists.append(RemoteDMATransfer(dst_ids=[dst(c) for c in far + near], dma_engine_mask=1 << eng[2 * e], remote_sem=s.kar,
-                                       srcs=[T.kd[2 * HALF - 2]], dsts=[T.kd[2 * slot(c) + e] for c in far + near]))
-        lists.append(RemoteDMATransfer(dst_ids=[dst(partner)] * HALF, dma_engine_mask=1 << eng[4 + 2 * e],
-                                       remote_sem=s.rar, srcs=[T.ld[e]], dsts=[T.rd[2 * q + e] for q in range(HALF)]))
+    g.wait_ge(s.ll, 64)
+    lists = [RemoteDMATransfer(dst_ids=[dst(c) for c in far + near], dma_engine_mask=1 << eng[0], remote_sem=s.kar,
+                               srcs=[T.kd[HALF - 1]], dsts=[T.kd[slot(c)] for c in far + near]),
+             RemoteDMATransfer(dst_ids=[dst(partner)] * HALF, dma_engine_mask=1 << eng[2], remote_sem=s.rar,
+                               srcs=[T.ld[:]], dsts=[T.rd[q] for q in range(HALF)])]
     g.remote_dma_fused(lists, local_sem=s.snt)
     sent[0] += len(lists)
     g.wait_ge(s.vq, 1)
@@ -120,11 +116,10 @@ def rank_program(g, core, T, topo):
     g.wait_ge(s.vp1, 1)
     send([partner], u8(T.sl[:, B:S]), [u8(T.arc[:, B:S])], s.ca1)
 
-    y.wait_ge(s.lc, 16)
-    y.wait_ge(s.kar, 2 * len(peers))
-    y.dma_start(T.kq[:, 0:8], T.kd[:, :, 0]).then_inc(s.kl, 16)
-    y.wait_ge(s.rar, 2 * HALF)
-    y.dma_start(T.kq[:, 8:16], T.rd[:, :, 0]).then_inc(s.kl, 16)
+    y.wait_ge(s.kar, len(peers))
+    y.dma_start(T.kq[:, 0:8], T.kd[:]).then_inc(s.kl, 16)
+    y.wait_ge(s.rar, HALF)
+    y.dma_start(T.kq[:, 8:16], T.rd[:]).then_inc(s.rl, 16)
     y.sem_inc(s.go, 1)
 
     fill = float(HALF * TC - MID)
@@ -137,16 +132,19 @@ def rank_program(g, core, T, topo):
     v.memset(T.tb[:, F1:FV], fill).then_inc(s.vt2, 1)
     v.wait_ge(s.wl, 16)
     v.quantize_mx(T.wq[:], T.wp[:], T.wt[:]).then_inc(s.vw, 1)
-    v.wait_ge(s.ol, 16 * HALF)
-    v.wait_ge(s.kl, 32)
-    v.tensor_scalar(T.kqa[:], T.kq[:], NK - 1, None, ALU.bitwise_and).then_inc(s.vka, 1)
+    v.wait_ge(s.kl, 16)
+    v.tensor_scalar(T.kqa[:, 0:8], T.kq[:, 0:8], NK - 1, None, ALU.bitwise_and).then_inc(s.vka, 1)
     v.wait_ge(s.vka, 1)
     v.tensor_copy(T.ko[:, 0:8], T.kqa[:, 0:8]).then_inc(s.vk, 1)
-    for h in range(2):
-        v.tensor_copy(T.ko[:, 8 + h:40:2], T.kqa[:, 8:24]).then_inc(s.vl, 1)
+    v.wait_ge(s.ol, 16 * HALF)
+    v.wait_ge(s.rl, 16)
+    v.tensor_scalar(T.kqa[:, 8:24], T.kq[:, 8:24], NK - 1, None, ALU.bitwise_and).then_inc(s.vla, 1)
     for q, n in ((s.vt0, 1), (s.vt1, 1), (s.vt2, 1), (s.af, 3), (s.ival, HALF), (s.vk, 1)):
         v.wait_ge(q, n)
     v.tensor_copy(T.tb[:].indirect(T.ko[:, 0:8]), T.vals[:]).then_inc(s.vsc, 1)
+    v.wait_ge(s.vla, 1)
+    for h in range(2):
+        v.tensor_copy(T.ko[:, 8 + h:40:2], T.kqa[:, 8:24]).then_inc(s.vl, 1)
     v.wait_ge(s.vl, 2)
     v.wait_ge(s.vsc, 1)
     v.tensor_copy(T.g1[:, 0:B], T.tb[:].indirect(T.ko[:, 8:16])).then_inc(s.vg1, 1)

from concourse.bass import DstId, RemoteDMATransfer
from concourse.mybir import dt, AluOpType, ActivationFunctionType

TC, S, O, NK = 128, 256, 2, 8192
HALF = 4
Z = 16
WIN = HALF * TC + Z
OWN = (HALF - 1) * TC
MID = 256
B = 128
F0, F1, FV = 512, 2048, 5504
FA = FV + F0 + (NK - FV - F0) // 2

SCRATCH = {
    "kd": ("dram", [HALF, 128, 2], "int32"),
    "ld": ("dram", [128, 2], "int32"),
    "rd": ("dram", [HALF, 128, 2], "int32"),
    "kq": ("sbuf", [128, 24], "int32"),
    "kqa": ("sbuf", [128, 24], "int32"),
    "ko": ("sbuf", [128, 40], "uint16"),
    "tb": ("sbuf", [128, NK], "bfloat16"),
    "vals": ("sbuf", [128, TC], "bfloat16"),
    "xt": ("sbuf", [128, 4 * (TC + Z)], "bfloat16"),
    "wt": ("sbuf", [128, 512 * O], "bfloat16"),
    "wq": ("sbuf", [128, 128 * O], "float8_e4m3fn_x4"),
    "wp": ("sbuf", [128, 128 * O], "uint8"),
    "win": ("sbuf", [128, WIN], "float8_e4m3fn_x4"),
    "sw": ("sbuf", [128, WIN], "uint8"),
    "sl": ("sbuf", [128, S], "float8_e4m3fn_x4"),
    "sp": ("sbuf", [128, S], "uint8"),
    "hc": ("sbuf", [128, S], "float8_e4m3fn_x4"),
    "hp": ("sbuf", [128, S], "uint8"),
    "arc": ("sbuf", [128, S], "float8_e4m3fn_x4"),
    "arp": ("sbuf", [128, S], "uint8"),
    "yb": ("sbuf", [128, O * S], "float32"),
    "ps": ("psum", [128, 2048], "float32"),
}
for n in (1, 2):
    SCRATCH["g%d" % n] = ("sbuf", [128, S], "bfloat16")
    SCRATCH["t%d" % n] = ("sbuf", [128, S], "bfloat16")
    SCRATCH["u%d" % n] = ("sbuf", [64, 16], "float32")
    SCRATCH["w%d" % n] = ("sbuf", [64, 16], "float32")
    SCRATCH["of%d" % n] = ("sbuf", [128, 16], "uint16")
SEMAPHORES = ["ll", "xl", "wl", "ol", "kl", "rl", "vla", "go", "kar", "rar", "car", "sar", "ca0", "ca1", "sa", "snt",
              "ival", "vz", "vt0", "vt1", "vt2", "af", "vq", "vw", "vka", "vk", "vl", "vsc", "vg1", "ag1", "ag2",
              "vt_1", "vu1", "vw1", "vo1", "vt_2", "vu2", "vw2", "vo2", "vp0", "vp1", "as1", "vh0", "vh1", "ah0", "ah1",
              "mm0", "mm1", "mm2", "mm3", "cp0", "cp1", "cp2", "cp3", "st"]


def rank_program(g, core, T, topo):
    if T.rank_of(core) is None:
        return
    s, v, a, p, y = T.sem, g.vector, g.scalar, g.tensor, g.sync
    ACT, ALU = ActivationFunctionType, AluOpType
    half = [c for c in T.cores if c == core or topo.same_plane(c, core)]
    partner = [c for c in T.cores if topo.mates(c, core)][0]

    def slot(c):
        return (half.index(c) ^ half.index(core)) - 1
    peers = sorted([c for c in half if c != core], key=slot)
    far, near = peers[:1], peers[1:]

    def dst(c):
        rid, pid = topo.addr(c, core)
        return DstId(rid=rid, pnc=pid)

    mask = topo.mask(core, partner)
    for c in peers:
        mask &= topo.mask(core, c)
    eng = [e for e in topo.engines(core, partner) if mask >> e & 1]
    ne = len(eng)
    sent = [0]

    def send(to, src, dsts, sem):
        g.remote_dma_fused([RemoteDMATransfer(dst_ids=[dst(c) for c in to], dma_engine_mask=mask, remote_sem=sem,
                                              srcs=[src], dsts=dsts)], local_sem=s.snt)
        sent[0] += ne

    def u8(view):
        return view.bitcast(dt.uint8)

    def u32(view):
        return view.bitcast(dt.uint32)

    for e, q in enumerate((y, a)):
        q.dma_start(T.ld[64 * e:64 * e + 64, :], T.lk[:, 8 * e:8 * e + 8]).then_inc(s.ll, 16)
        q.dma_start(T.kd[HALF - 1, 64 * e:64 * e + 64, :], T.ky[:]).then_inc(s.ll, 16)
    y.dma_start(T.xt[:, 0:4 * TC], T.x[:]).then_inc(s.xl, 16)
    y.dma_start(T.wt[:], T.w[:]).then_inc(s.wl, 16)
    y.wait_ge(s.ll, 64)
    for q in range(HALF):
        y.dma_start(T.kq[32 * q:32 * q + 32, 16:24], T.ld[:]).then_inc(s.ol, 16)

    def vals(q):
        g.iota(T.vals[32 * q:32 * q + 32, :], [[1, TC]], TC * q - MID, 0, allow_small_or_imprecise_dtypes=True).then_inc(s.ival, 1)
    vals(0)
    vals(1)
    g.wait_ge(s.ll, 64)
    lists = [RemoteDMATransfer(dst_ids=[dst(c) for c in far + near], dma_engine_mask=1 << eng[0], remote_sem=s.kar,
                               srcs=[T.kd[HALF - 1]], dsts=[T.kd[slot(c)] for c in far + near]),
             RemoteDMATransfer(dst_ids=[dst(partner)] * HALF, dma_engine_mask=1 << eng[2], remote_sem=s.rar,
                               srcs=[T.ld[:]], dsts=[T.rd[q] for q in range(HALF)])]
    g.remote_dma_fused(lists, local_sem=s.snt)
    sent[0] += len(lists)
    g.wait_ge(s.vq, 1)
    send(far, u8(T.win[:, OWN:OWN + TC]), [u8(T.win[:, TC * slot(c):TC * slot(c) + TC]) for c in far], s.car)
    vals(2)
    vals(3)
    g.wait_ge(s.go, 1)
    send(near, u8(T.win[:, OWN:OWN + TC]), [u8(T.win[:, TC * slot(c):TC * slot(c) + TC]) for c in near], s.car)
    send(far + near, T.sw[:, OWN:OWN + TC], [T.sw[:, TC * slot(c):TC * slot(c) + TC] for c in far + near], s.sar)
    g.wait_ge(s.vp0, 1)
    send([partner], u8(T.sl[:, 0:B]), [u8(T.arc[:, 0:B])], s.ca0)
    g.wait_ge(s.as1, 2)
    send([partner], T.sp[:], [T.arp[:]], s.sa)
    g.wait_ge(s.vp1, 1)
    send([partner], u8(T.sl[:, B:S]), [u8(T.arc[:, B:S])], s.ca1)

    y.wait_ge(s.kar, len(peers))
    y.dma_start(T.kq[:, 0:8], T.kd[:]).then_inc(s.kl, 16)
    y.wait_ge(s.rar, HALF)
    y.dma_start(T.kq[:, 8:16], T.rd[:]).then_inc(s.rl, 16)
    y.sem_inc(s.go, 1)

    fill = float(HALF * TC - MID)
    v.memset(T.tb[:, 0:F0], fill).then_inc(s.vt0, 1)
    v.memset(T.xt[:, 4 * TC:4 * (TC + Z)], 0.0).then_inc(s.vz, 1)
    v.memset(T.tb[:, F0:F1], fill).then_inc(s.vt1, 1)
    v.wait_ge(s.vz, 1)
    v.wait_ge(s.xl, 16)
    v.quantize_mx(T.win[:, OWN:WIN], T.sw[:, OWN:WIN], T.xt[:]).then_inc(s.vq, 1)
    v.memset(T.tb[:, F1:FV], fill).then_inc(s.vt2, 1)
    v.wait_ge(s.wl, 16)
    v.quantize_mx(T.wq[:], T.wp[:], T.wt[:]).then_inc(s.vw, 1)
    v.wait_ge(s.kl, 16)
    v.tensor_scalar(T.kqa[:, 0:8], T.kq[:, 0:8], NK - 1, None, ALU.bitwise_and).then_inc(s.vka, 1)
    v.wait_ge(s.vka, 1)
    v.tensor_copy(T.ko[:, 0:8], T.kqa[:, 0:8]).then_inc(s.vk, 1)
    v.wait_ge(s.ol, 16 * HALF)
    v.wait_ge(s.rl, 16)
    v.tensor_scalar(T.kqa[:, 8:24], T.kq[:, 8:24], NK - 1, None, ALU.bitwise_and).then_inc(s.vla, 1)
    for q, n in ((s.vt0, 1), (s.vt1, 1), (s.vt2, 1), (s.af, 3), (s.ival, HALF), (s.vk, 1)):
        v.wait_ge(q, n)
    v.tensor_copy(T.tb[:].indirect(T.ko[:, 0:8]), T.vals[:]).then_inc(s.vsc, 1)
    v.wait_ge(s.vla, 1)
    for h in range(2):
        v.tensor_copy(T.ko[:, 8 + h:40:2], T.kqa[:, 8:24]).then_inc(s.vl, 1)
    v.wait_ge(s.vl, 2)
    v.wait_ge(s.vsc, 1)
    v.tensor_copy(T.g1[:, 0:B], T.tb[:].indirect(T.ko[:, 8:16])).then_inc(s.vg1, 1)

    def turn(n):
        v.transpose(T["t%d" % n][:], T["g%d" % n][:]).then_inc(s["vt_%d" % n], 1)

    def offsets(n):
        t, u, w, of = T["t%d" % n], T["u%d" % n], T["w%d" % n], T["of%d" % n]
        v.wait_ge(s["vt_%d" % n], 1)
        for e in range(2):
            v.tensor_tensor(u[:, 8 * e:8 * e + 8], t[0:64, 16 * e:S:32], t[64:128, 16 * e:S:32], ALU.min).then_inc(s["vu%d" % n], 1)
        v.wait_ge(s["vu%d" % n], 2)
        for h in range(2):
            v.tensor_tensor(w[32 * h:32 * h + 32, :], u[0:32, :], u[32:64, :], ALU.min).then_inc(s["vw%d" % n], 1)
        v.wait_ge(s["vw%d" % n], 2)
        for h in range(2):
            v.tensor_scalar(of[64 * h:64 * h + 64, :], w[:], float(MID), None, ALU.add).then_inc(s["vo%d" % n], 1)
        v.wait_ge(s["vo%d" % n], 2)

    def pick(out, of, h):
        return v.tensor_copy(u32(out[:, B * h:B * h + B]), u32(T.win[:]).indirect(of[:, 8 * h:8 * h + 8]))

    v.wait_ge(s.vg1, 1)
    v.wait_ge(s.ag1, 1)
    turn(1)
    offsets(1)
    v.wait_ge(s.vq, 1)
    v.wait_ge(s.car, ne * len(peers))
    pick(T.sl, T.of1, 0).then_inc(s.vp0, 1)
    v.wait_ge(s.ag2, 1)
    turn(2)
    pick(T.sl, T.of1, 1).then_inc(s.vp1, 1)
    offsets(2)
    for h in range(2):
        pick(T.hc, T.of2, h).then_inc(s["vh%d" % h], 1)

    a.wait_ge(s.vt0, 1)
    a.activation(T.tb[:, FV:FV + F0], T.tb[:, 0:F0], ACT.Copy).then_inc(s.af, 1)
    a.wait_ge(s.vt1, 1)
    a.activation(T.tb[:, FV + F0:FA], T.tb[:, 0:FA - FV - F0], ACT.Copy).then_inc(s.af, 1)
    a.activation(T.tb[:, FA:NK], T.tb[:, 0:NK - FA], ACT.Copy).then_inc(s.af, 1)
    a.wait_ge(s.vl, 2)
    a.wait_ge(s.vsc, 1)
    a.activation(T.g1[:, B:S], T.tb[:].indirect(T.ko[:, 16:24]), ACT.Copy).then_inc(s.ag1, 1)
    a.activation(T.g2[:], T.tb[:].indirect(T.ko[:, 24:40]), ACT.Copy).then_inc(s.ag2, 1)

    def pick_scales(out, of, h):
        return a.activation(out[:, B * h:B * h + B], T.sw[:].indirect(of[:, 8 * h:8 * h + 8]), ACT.Copy)
    a.wait_ge(s.vq, 1)
    a.wait_ge(s.sar, ne * len(peers))
    a.wait_ge(s.vo1, 2)
    for h in range(2):
        pick_scales(T.sp, T.of1, h).then_inc(s.as1, 1)
    a.wait_ge(s.vo2, 2)
    for h in range(2):
        pick_scales(T.hp, T.of2, h).then_inc(s["ah%d" % h], 1)

    def product(o, h, codes, scales, first):
        q = 2 * h + o
        return p.matmul_mx(T.ps[:, 512 * q:512 * q + B], T.wq[:, 128 * o:128 * o + 128], T.wp[:, 128 * o:128 * o + 128],
                           codes[:, B * h:B * h + B], scales[:, B * h:B * h + B], first, not first)
    p.wait_ge(s.vw, 1)
    for h in range(2):
        p.wait_ge(s["vh%d" % h], 1)
        p.wait_ge(s["ah%d" % h], 1)
        for o in range(O):
            product(o, h, T.hc, T.hp, True)
        p.wait_ge(s["ca%d" % h], ne)
        if h == 0:
            p.wait_ge(s.sa, ne)
        for o in range(O):
            product(o, h, T.arc, T.arp, False).then_inc(s["mm%d" % (2 * h + o)], 1)
    for q in range(2 * O):
        h, o = q // 2, q % 2
        out = T.yb[:, S * o + B * h:S * o + B * h + B]
        if o == 0:
            v.wait_ge(s["mm%d" % q], 1)
            v.tensor_copy(out, T.ps[:, 512 * q:512 * q + B]).then_inc(s["cp%d" % q], 1)
        else:
            a.wait_ge(s["mm%d" % q], 1)
            a.activation(out, T.ps[:, 512 * q:512 * q + B], ACT.Copy).then_inc(s["cp%d" % q], 1)
        z = a if q == 2 * O - 1 else y
        z.wait_ge(s["cp%d" % q], 1)
        z.dma_start(T.y[:, S * o + B * h:S * o + B * h + B], out).then_inc(s.st, 16)
    y.wait_ge(s.st, 32 * O)
    g.wait_ge(s.snt, sent[0])
